import numpy as np
import ml_dtypes


def mxq(x, axis, fmt="e4m3"):
    dtype, down = {"e4m3": (ml_dtypes.float8_e4m3fn, 7), "e5m2": (ml_dtypes.float8_e5m2, 14)}[fmt]
    v = np.moveaxis(np.asarray(x, np.float32).astype(ml_dtypes.bfloat16).astype(np.float64), axis, -1)
    blocks = v.reshape(v.shape[:-1] + (-1, 32))
    amax = np.abs(blocks).max(-1, keepdims=True)
    byte = np.maximum(np.where(amax > 0, np.frexp(amax)[1] - 1 + 127, 0) - down, 1)
    scale = np.exp2(byte - 127.0)
    codes = (blocks / scale).astype(np.float32).astype(dtype).astype(np.float64)
    return np.moveaxis((codes * scale).reshape(v.shape), -1, axis)


WIDE = False


def mx_kscale(k):
    if not WIDE:
        return np.ones(k)
    levels = np.array([10, -10, 5, -5, 0])
    if k % 512:
        return np.exp2(np.random.permutation(np.resize(levels, k // 32))).repeat(32)
    a = np.empty((k // 512, 16))
    for p in range(k // 512):
        a[p, :8] = np.random.permutation(np.resize(levels, 8))
        for g in range(8):
            far = levels[np.abs(levels - a[p, g]) >= 10]
            a[p, g + 8] = far[np.random.randint(len(far))]
    return np.exp2(a.ravel()).repeat(32)


def f64(x):
    return np.asarray(x).astype(np.float64)


def striped(idx):
    return np.tile(idx.reshape(-1, 16).T, (8, 1)).astype(np.uint16)


def unstriped(offs):
    return offs[:16].T.reshape(-1).astype(np.int64)


K, T, E, C, N = 1024, 1536, 4, 256, 512


def by_expert(wq, xq):
    return np.concatenate([wq[e].T @ xq[:, e * C:(e + 1) * C] for e in range(E)], axis=1)


def setup_inputs():
    n = np.random.standard_normal
    s = mx_kscale(K)[:, None]
    return {
        "xT": (n((K, T)) * s).astype(np.float32),
        "xr": n((N, T)).astype(np.float32),
        "w": (n((E, K, N)) / np.sqrt(K) / s[None]).astype(np.float32),
        "gate": np.tile(np.random.uniform(0.2, 1.0, E * C), (N, 1)).astype(np.float32),
        "offs": striped(np.random.permutation(T)[:E * C]),
    }


def reference(xT, xr, w, gate, offs):
    idx = unstriped(offs)
    xq = mxq(f64(xT)[:, idx], 0, "e4m3")
    y = by_expert(mxq(f64(w), 1, "e4m3"), xq)
    out = f64(xr).copy()
    out[:, idx] += f64(gate) * y
    return out

@@ -1,0 +1,199 @@
+from contextlib import ExitStack
+
+import concourse.mybir as mybir
+
+K, T, E, C, N = 1024, 1536, 4, 256, 512
+S = E * C
+FLOPS = 2 * K * S * N
+
+F32 = mybir.dt.float32
+BF16 = mybir.dt.bfloat16
+U32 = mybir.dt.uint32
+U16 = mybir.dt.uint16
+U8 = mybir.dt.uint8
+FP8X4 = mybir.dt.float8_e4m3fn_x4
+MULT = mybir.AluOpType.mult
+ADD = mybir.AluOpType.add
+
+P = 128
+PACK = 4
+KP = P * PACK
+PASSES = K // KP
+XC = 512
+NT = N // P
+VX = [256, 0, 0, 0, 0, 192]
+VW = [0, 0, 0, 0, 96]
+PIECES = [(0, 0, 256), (0, 256, 512), (1, 0, 512), (2, 0, 512), (3, 0, 512)]
+
+
+def interleave(copy, dst, src, a, b):
+    if a < b:
+        copy(
+            out=dst[:, a:b, :].rearrange("p (c i) j -> p c j i", i=4),
+            in_=src[:, :, a:b].rearrange("p j (c i) -> p c j i", i=4),
+        )
+
+
+def tile_moe_res_lin_none_kernel(tc, xT, xr, w, gate, offs, out):
+    nc = tc.nc
+    with ExitStack() as ctx:
+        keep = ctx.enter_context(tc.tile_pool(name="keep", bufs=1))
+        xraw = ctx.enter_context(tc.tile_pool(name="xraw", bufs=4))
+        xgrp = ctx.enter_context(tc.tile_pool(name="xgrp", bufs=3))
+        wraw = ctx.enter_context(tc.tile_pool(name="wraw", bufs=7))
+        wgrp = ctx.enter_context(tc.tile_pool(name="wgrp", bufs=3))
+        wq = ctx.enter_context(tc.tile_pool(name="wq", bufs=4))
+        yp = ctx.enter_context(tc.tile_pool(name="yp", bufs=4))
+        psum = ctx.enter_context(tc.psum_pool(name="psum", bufs=8))
+
+        offsets = keep.tile([P, S // 16], U16, name="offsets")
+        nc.sync.dma_start(offsets[:], offs)
+
+        x_codes = [keep.tile([P, T], U32, name=f"x_codes{c}", align_bytes=64) for c in range(PASSES)]
+        x_scales = keep.tile([P, T], U8, name="x_scales", align_bytes=64)
+        g_codes = [keep.tile([P, S], U32, name=f"g_codes{c}", align_bytes=64) for c in range(PASSES)]
+        g_scales = keep.tile([P, S], U8, name="g_scales", align_bytes=64)
+        window = [keep.tile([P, T], F32, name=f"window{t}") for t in range(NT)]
+        res = [keep.tile([P, T], F32, name=f"res{t}") for t in range(NT)]
+        gates = [keep.tile([P, NT, S // 2], F32, name=f"gates{h}") for h in range(2)]
+
+        nc.gpsimd.memset(x_scales[:], 0)
+        for t in range(NT):
+            nc.gpsimd.memset(window[t][:], 0.0)
+
+        pending = None
+
+        def quantise_x(c, t, grouped):
+            cols = slice(t * XC, (t + 1) * XC)
+            nc.vector.quantize_mx(
+                out=x_codes[c][:, cols].bitcast(FP8X4),
+                scales=x_scales[4 * c :, cols],
+                in_=grouped[:].rearrange("p w j -> p (w j)"),
+            )
+
+        for c in range(PASSES):
+            for t in range(T // XC):
+                raw = xraw.tile([P, PACK, XC], F32, name="x_raw")
+                nc.sync.dma_start(
+                    raw[:],
+                    xT[c * KP : (c + 1) * KP, t * XC : (t + 1) * XC].rearrange("(p j) w -> p j w", j=PACK),
+                )
+                grouped = xgrp.tile([P, XC, PACK], BF16, name="x_grouped", align_bytes=64)
+                v = VX[c * 3 + t]
+                interleave(nc.vector.tensor_copy, grouped, raw, 0, v)
+                interleave(nc.scalar.copy, grouped, raw, v, XC)
+                if pending:
+                    quantise_x(*pending)
+                pending = (c, t, grouped)
+        quantise_x(*pending)
+        nc.vector.tensor_copy(g_codes[0][:], x_codes[0][:].indirect(offsets[:]))
+        nc.vector.tensor_copy(g_scales[:], x_scales[:].indirect(offsets[:]))
+        nc.vector.tensor_copy(g_codes[1][:], x_codes[1][:].indirect(offsets[:]))
+
+        def load_gates(h):
+            nc.sync.dma_start(
+                gates[h][:],
+                gate[:, h * S // 2 : (h + 1) * S // 2].rearrange("(t p) s -> p t s", p=P),
+            )
+
+        def load_res(t):
+            nc.sync.dma_start(res[t][:], xr[t * P : (t + 1) * P, :])
+
+        def finish(engine, t):
+            engine.tensor_tensor(res[t][:], window[t][:], res[t][:], ADD)
+            nc.sync.dma_start(out[t * P : (t + 1) * P, :], res[t][:])
+
+        def load_w(e, lo, hi):
+            raws = []
+            for c in range(PASSES):
+                raw = wraw.tile([P, PACK, hi - lo], F32, name="w_raw")
+                nc.sync.dma_start(
+                    raw[:], w[e, c * KP : (c + 1) * KP, lo:hi].rearrange("(p j) n -> p j n", j=PACK)
+                )
+                raws.append(raw)
+            return raws
+
+        def front(raws, width, v):
+            codes = wq.tile([P, PASSES, width], U32, name="w_codes", align_bytes=64)
+            scales = wq.tile([P, PASSES, width], U8, name="w_scales", align_bytes=64)
+            for c in range(PASSES):
+                grouped = wgrp.tile([P, width, PACK], BF16, name="w_grouped", align_bytes=64)
+                interleave(nc.vector.tensor_copy, grouped, raws[c], 0, v)
+                interleave(nc.scalar.copy, grouped, raws[c], v, width)
+                nc.vector.quantize_mx(
+                    out=codes[:, c, :].bitcast(FP8X4),
+                    scales=scales[:, c, :],
+                    in_=grouped[:].rearrange("p w j -> p (w j)"),
+                )
+            return codes, scales
+
+        def multiply(acc, e, t, tiles):
+            codes, scales, lo = tiles
+            slots = slice(e * C, (e + 1) * C)
+            n_cols = slice(t * P - lo, (t + 1) * P - lo)
+            for c in range(PASSES):
+                nc.tensor.matmul_mx(
+                    out=acc,
+                    lhsT=codes[:, c, n_cols].bitcast(FP8X4),
+                    lhsT_scale=scales[:, c, n_cols],
+                    rhs=g_codes[c][:, slots].bitcast(FP8X4),
+                    rhs_scale=g_scales[4 * c :, slots],
+                    start=(c == 0),
+                    stop=(c == PASSES - 1),
+                )
+
+        def gated_two_tiles(e, t0, tiles):
+            acc = psum.tile([P, 2, C], F32, name="acc")
+            for i in range(2):
+                multiply(acc[:, i, :], e, t0 + i, tiles)
+            y = yp.tile([P, 2, C], F32, name="y")
+            g_cols = slice((e % 2) * C, (e % 2 + 1) * C)
+            nc.vector.tensor_tensor(y[:], acc[:], gates[e // 2][:, t0 : t0 + 2, g_cols], MULT)
+            return [(t0 + i, e * C, C, y[:, i, :]) for i in range(2)]
+
+        def gated_two_experts(e0, t, tiles):
+            acc = psum.tile([P, 2, C], F32, name="acc")
+            for i in range(2):
+                multiply(acc[:, i, :], e0 + i, t, tiles[i])
+            y = yp.tile([P, 2, C], F32, name="y")
+            nc.vector.tensor_tensor(y[:].rearrange("p e s -> p (e s)"), acc[:].rearrange("p e s -> p (e s)"), gates[e0 // 2][:, t, :], MULT)
+            return [(t, e0 * C, 2 * C, y[:].rearrange("p e s -> p (e s)"))]
+
+        def scatter(items):
+            for t, slot, count, values in items:
+                nc.vector.tensor_copy(window[t][:].indirect(offsets[:, slot // 16 : (slot + count) // 16]), values)
+
+        raws = []
+        for k, piece in enumerate(PIECES):
+            raws.append(load_w(*piece))
+            if k == 1:
+                load_gates(0)
+            if k == 2:
+                load_gates(1)
+        for t in range(NT):
+            load_res(t)
+
+        def quantise_w(k):
+            e, lo, hi = PIECES[k]
+            return front(raws[k], hi - lo, VW[k]) + (lo,)
+
+        w0a = quantise_w(0)
+        w0b = quantise_w(1)
+        a = gated_two_tiles(0, 0, w0a)
+        w1 = quantise_w(2)
+        b = gated_two_tiles(0, 2, w0b)
+        scatter(a)
+        a = gated_two_tiles(1, 0, w1)
+        scatter(b)
+        w2 = quantise_w(3)
+        b = gated_two_tiles(1, 2, w1)
+        scatter(a)
+        w3 = quantise_w(4)
+        a = gated_two_experts(2, 0, (w2, w3))
+        scatter(b)
+        for t in range(NT):
+            b = a
+            if t + 1 < NT:
+                a = gated_two_experts(2, t + 1, (w2, w3))
+            scatter(b)
+            finish(nc.vector if t == NT - 1 else nc.gpsimd, t)

@@ -21,29 +21,17 @@ KP = P * PACK
 PASSES = K // KP
 XC = 512
 NT = N // P
-VX = [256, 0, 0, 0, 0, 192]
-VW = [0, 0, 0, 0, 96]
-PIECES = [(0, 0, 256), (0, 256, 512), (1, 0, 512), (2, 0, 512), (3, 0, 512)]
-
-
-def interleave(copy, dst, src, a, b):
-    if a < b:
-        copy(
-            out=dst[:, a:b, :].rearrange("p (c i) j -> p c j i", i=4),
-            in_=src[:, :, a:b].rearrange("p j (c i) -> p c j i", i=4),
-        )
 
 
 def tile_moe_res_lin_none_kernel(tc, xT, xr, w, gate, offs, out):
     nc = tc.nc
     with ExitStack() as ctx:
         keep = ctx.enter_context(tc.tile_pool(name="keep", bufs=1))
-        xraw = ctx.enter_context(tc.tile_pool(name="xraw", bufs=4))
-        xgrp = ctx.enter_context(tc.tile_pool(name="xgrp", bufs=3))
-        wraw = ctx.enter_context(tc.tile_pool(name="wraw", bufs=7))
-        wgrp = ctx.enter_context(tc.tile_pool(name="wgrp", bufs=3))
+        stage = ctx.enter_context(tc.tile_pool(name="stage", bufs=12))
+        groups = ctx.enter_context(tc.tile_pool(name="groups", bufs=5))
         wq = ctx.enter_context(tc.tile_pool(name="wq", bufs=4))
-        yp = ctx.enter_context(tc.tile_pool(name="yp", bufs=4))
+        yp = ctx.enter_context(tc.tile_pool(name="yp", bufs=5))
+        zp = ctx.enter_context(tc.tile_pool(name="zp", bufs=3))
         psum = ctx.enter_context(tc.psum_pool(name="psum", bufs=8))
 
         offsets = keep.tile([P, S // 16], U16, name="offsets")
@@ -54,146 +42,174 @@ def tile_moe_res_lin_none_kernel(tc, xT, xr, w, gate, offs, out):
         g_codes = [keep.tile([P, S], U32, name=f"g_codes{c}", align_bytes=64) for c in range(PASSES)]
         g_scales = keep.tile([P, S], U8, name="g_scales", align_bytes=64)
         window = [keep.tile([P, T], F32, name=f"window{t}") for t in range(NT)]
-        res = [keep.tile([P, T], F32, name=f"res{t}") for t in range(NT)]
-        gates = [keep.tile([P, NT, S // 2], F32, name=f"gates{h}") for h in range(2)]
+        gates = [keep.tile([P, NT, C], F32, name=f"gates{e}") for e in range(E)]
+        res = {}
 
         nc.gpsimd.memset(x_scales[:], 0)
         for t in range(NT):
             nc.gpsimd.memset(window[t][:], 0.0)
 
-        pending = None
-
-        def quantise_x(c, t, grouped):
-            cols = slice(t * XC, (t + 1) * XC)
-            nc.vector.quantize_mx(
-                out=x_codes[c][:, cols].bitcast(FP8X4),
-                scales=x_scales[4 * c :, cols],
-                in_=grouped[:].rearrange("p w j -> p (w j)"),
-            )
-
-        for c in range(PASSES):
-            for t in range(T // XC):
-                raw = xraw.tile([P, PACK, XC], F32, name="x_raw")
-                nc.sync.dma_start(
-                    raw[:],
-                    xT[c * KP : (c + 1) * KP, t * XC : (t + 1) * XC].rearrange("(p j) w -> p j w", j=PACK),
-                )
-                grouped = xgrp.tile([P, XC, PACK], BF16, name="x_grouped", align_bytes=64)
-                v = VX[c * 3 + t]
-                interleave(nc.vector.tensor_copy, grouped, raw, 0, v)
-                interleave(nc.scalar.copy, grouped, raw, v, XC)
-                if pending:
-                    quantise_x(*pending)
-                pending = (c, t, grouped)
-        quantise_x(*pending)
-        nc.vector.tensor_copy(g_codes[0][:], x_codes[0][:].indirect(offsets[:]))
-        nc.vector.tensor_copy(g_scales[:], x_scales[:].indirect(offsets[:]))
-        nc.vector.tensor_copy(g_codes[1][:], x_codes[1][:].indirect(offsets[:]))
-
-        def load_gates(h):
+        def load_x(c, t):
+            raw = stage.tile([P, PACK, XC], F32, name="raw")
             nc.sync.dma_start(
-                gates[h][:],
-                gate[:, h * S // 2 : (h + 1) * S // 2].rearrange("(t p) s -> p t s", p=P),
+                raw[:],
+                xT[c * KP : (c + 1) * KP, t * XC : (t + 1) * XC].rearrange("(p j) w -> p j w", j=PACK),
             )
-
-        def load_res(t):
-            nc.sync.dma_start(res[t][:], xr[t * P : (t + 1) * P, :])
-
-        def finish(engine, t):
-            engine.tensor_tensor(res[t][:], window[t][:], res[t][:], ADD)
-            nc.sync.dma_start(out[t * P : (t + 1) * P, :], res[t][:])
+            return raw
 
         def load_w(e, lo, hi):
             raws = []
             for c in range(PASSES):
-                raw = wraw.tile([P, PACK, hi - lo], F32, name="w_raw")
+                raw = stage.tile([P, PACK, hi - lo], F32, name="raw")
                 nc.sync.dma_start(
                     raw[:], w[e, c * KP : (c + 1) * KP, lo:hi].rearrange("(p j) n -> p j n", j=PACK)
                 )
                 raws.append(raw)
             return raws
 
-        def front(raws, width, v):
-            codes = wq.tile([P, PASSES, width], U32, name="w_codes", align_bytes=64)
-            scales = wq.tile([P, PASSES, width], U8, name="w_scales", align_bytes=64)
-            for c in range(PASSES):
-                grouped = wgrp.tile([P, width, PACK], BF16, name="w_grouped", align_bytes=64)
-                interleave(nc.vector.tensor_copy, grouped, raws[c], 0, v)
-                interleave(nc.scalar.copy, grouped, raws[c], v, width)
-                nc.vector.quantize_mx(
-                    out=codes[:, c, :].bitcast(FP8X4),
-                    scales=scales[:, c, :],
-                    in_=grouped[:].rearrange("p w j -> p (w j)"),
-                )
-            return codes, scales
+        def load_gate(e):
+            nc.sync.dma_start(gates[e][:], gate[:, e * C : (e + 1) * C].rearrange("(t p) s -> p t s", p=P))
 
-        def multiply(acc, e, t, tiles):
+        def load_res(t):
+            res[t] = stage.tile([P, T], F32, name="raw")
+            nc.sync.dma_start(res[t][:], xr[t * P : (t + 1) * P, :])
+
+        def interleave(raw, width, v):
+            grouped = groups.tile([P, width, PACK], BF16, name="grouped", align_bytes=64)
+            for copy, a, b in ((nc.vector.tensor_copy, 0, v), (nc.scalar.copy, v, width)):
+                if a < b:
+                    copy(
+                        out=grouped[:, a:b, :].rearrange("p (c i) j -> p c j i", i=4),
+                        in_=raw[:, :, a:b].rearrange("p j (c i) -> p c j i", i=4),
+                    )
+            return grouped
+
+        def quantise(codes, scales, grouped):
+            nc.vector.quantize_mx(
+                out=codes.bitcast(FP8X4), scales=scales, in_=grouped[:].rearrange("p w j -> p (w j)")
+            )
+
+        def quantise_x(c, t, grouped):
+            cols = slice(t * XC, (t + 1) * XC)
+            quantise(x_codes[c][:, cols], x_scales[4 * c :, cols], grouped)
+
+        def gather(dst, src, lo, hi):
+            nc.vector.tensor_copy(dst[:, lo:hi], src[:].indirect(offsets[:, lo // 16 : hi // 16]))
+
+        def quantise_w(lo, hi, grouped):
+            codes = wq.tile([P, PASSES, hi - lo], U32, name="w_codes", align_bytes=64)
+            scales = wq.tile([P, PASSES, hi - lo], U8, name="w_scales", align_bytes=64)
+            for c in range(PASSES):
+                quantise(codes[:, c, :], scales[:, c, :], grouped[c])
+            return codes, scales, lo
+
+        def multiply(e, t0, tiles):
+            acc = psum.tile([P, 2, C], F32, name="acc")
             codes, scales, lo = tiles
             slots = slice(e * C, (e + 1) * C)
-            n_cols = slice(t * P - lo, (t + 1) * P - lo)
-            for c in range(PASSES):
-                nc.tensor.matmul_mx(
-                    out=acc,
-                    lhsT=codes[:, c, n_cols].bitcast(FP8X4),
-                    lhsT_scale=scales[:, c, n_cols],
-                    rhs=g_codes[c][:, slots].bitcast(FP8X4),
-                    rhs_scale=g_scales[4 * c :, slots],
-                    start=(c == 0),
-                    stop=(c == PASSES - 1),
-                )
-
-        def gated_two_tiles(e, t0, tiles):
-            acc = psum.tile([P, 2, C], F32, name="acc")
             for i in range(2):
-                multiply(acc[:, i, :], e, t0 + i, tiles)
-            y = yp.tile([P, 2, C], F32, name="y")
-            g_cols = slice((e % 2) * C, (e % 2 + 1) * C)
-            nc.vector.tensor_tensor(y[:], acc[:], gates[e // 2][:, t0 : t0 + 2, g_cols], MULT)
-            return [(t0 + i, e * C, C, y[:, i, :]) for i in range(2)]
+                n_cols = slice((t0 + i) * P - lo, (t0 + i + 1) * P - lo)
+                for c in range(PASSES):
+                    nc.tensor.matmul_mx(
+                        out=acc[:, i, :],
+                        lhsT=codes[:, c, n_cols].bitcast(FP8X4),
+                        lhsT_scale=scales[:, c, n_cols],
+                        rhs=g_codes[c][:, slots].bitcast(FP8X4),
+                        rhs_scale=g_scales[4 * c :, slots],
+                        start=(c == 0),
+                        stop=(c == PASSES - 1),
+                    )
+            return acc
 
-        def gated_two_experts(e0, t, tiles):
-            acc = psum.tile([P, 2, C], F32, name="acc")
-            for i in range(2):
-                multiply(acc[:, i, :], e0 + i, t, tiles[i])
+        def gated(e, t0, acc, how):
             y = yp.tile([P, 2, C], F32, name="y")
-            nc.vector.tensor_tensor(y[:].rearrange("p e s -> p (e s)"), acc[:].rearrange("p e s -> p (e s)"), gates[e0 // 2][:, t, :], MULT)
-            return [(t, e0 * C, 2 * C, y[:].rearrange("p e s -> p (e s)"))]
+            g = gates[e][:, t0 : t0 + 2, :]
+            if how == "v":
+                nc.vector.tensor_tensor(y[:], acc[:], g, MULT)
+            elif how == "d":
+                nc.scalar.copy(y[:], acc[:])
+            else:
+                z = zp.tile([P, 2, C], F32, name="z")
+                nc.scalar.copy(z[:], acc[:])
+                nc.gpsimd.tensor_tensor(y[:], z[:], g, MULT)
+            return [(e, t0 + i, y[:, i, :], how) for i in range(2)]
 
         def scatter(items):
-            for t, slot, count, values in items:
-                nc.vector.tensor_copy(window[t][:].indirect(offsets[:, slot // 16 : (slot + count) // 16]), values)
+            for e, t, values, how in items:
+                spots = window[t][:].indirect(offsets[:, e * C // 16 : (e + 1) * C // 16])
+                if how == "d":
+                    nc.vector.tensor_tensor(spots, values, gates[e][:, t, :], MULT)
+                else:
+                    nc.vector.tensor_copy(spots, values)
 
-        raws = []
-        for k, piece in enumerate(PIECES):
-            raws.append(load_w(*piece))
-            if k == 1:
-                load_gates(0)
-            if k == 2:
-                load_gates(1)
+        def finish(engine, t):
+            engine.tensor_tensor(res[t][:], window[t][:], res[t][:], ADD)
+            nc.sync.dma_start(out[t * P : (t + 1) * P, :], res[t][:])
+
+        x_at = [(c, t) for c in range(PASSES) for t in range(T // XC)]
+        x_raw = [load_x(c, t) for c, t in x_at]
+        w_raw = {}
+        w_raw[0] = load_w(0, 0, 256)
+        load_gate(0)
+        w_raw[1] = load_w(0, 256, 512)
+        w_raw[2] = load_w(1, 0, 512)
+        load_gate(1)
+        before = None
+        for i in range(len(x_at)):
+            grouped = interleave(x_raw[i], XC, [256, 128, 128, 128, 128, 192][i])
+            if before:
+                quantise_x(*before)
+            before = (*x_at[i], grouped)
+            if i == 3:
+                gather(g_codes[0], x_codes[0], 0, S)
+                w_raw[3] = load_w(2, 0, 512)
+                load_gate(2)
+            if i == 5:
+                w_raw[4] = load_w(3, 0, 512)
+                load_gate(3)
+        quantise_x(*before)
+        gather(g_scales, x_scales, 0, C)
+        gather(g_codes[1], x_codes[1], 0, C)
+
+        def group_w(k, lo, hi, v):
+            return [interleave(w_raw[k][c], hi - lo, v) for c in range(PASSES)]
+
+        g = group_w(0, 0, 256, 64)
+        w0a = quantise_w(0, 256, g)
+        u00 = gated(0, 0, multiply(0, 0, w0a), "v")
+        g = group_w(1, 256, 512, 0)
         for t in range(NT):
             load_res(t)
-
-        def quantise_w(k):
-            e, lo, hi = PIECES[k]
-            return front(raws[k], hi - lo, VW[k]) + (lo,)
-
-        w0a = quantise_w(0)
-        w0b = quantise_w(1)
-        a = gated_two_tiles(0, 0, w0a)
-        w1 = quantise_w(2)
-        b = gated_two_tiles(0, 2, w0b)
-        scatter(a)
-        a = gated_two_tiles(1, 0, w1)
-        scatter(b)
-        w2 = quantise_w(3)
-        b = gated_two_tiles(1, 2, w1)
-        scatter(a)
-        w3 = quantise_w(4)
-        a = gated_two_experts(2, 0, (w2, w3))
-        scatter(b)
-        for t in range(NT):
-            b = a
-            if t + 1 < NT:
-                a = gated_two_experts(2, t + 1, (w2, w3))
-            scatter(b)
-            finish(nc.vector if t == NT - 1 else nc.gpsimd, t)
+        w0b = quantise_w(256, 512, g)
+        gather(g_scales, x_scales, C, 2 * C)
+        gather(g_codes[1], x_codes[1], C, 2 * C)
+        u02 = gated(0, 2, multiply(0, 2, w0b), "g")
+        scatter(u00)
+        g = group_w(2, 0, 512, 0)
+        gather(g_scales, x_scales, 2 * C, 4 * C)
+        gather(g_codes[1], x_codes[1], 2 * C, 4 * C)
+        w1 = quantise_w(0, 512, g)
+        u10 = gated(1, 0, multiply(1, 0, w1), "g")
+        scatter(u02)
+        u12 = gated(1, 2, multiply(1, 2, w1), "g")
+        g = group_w(3, 0, 512, 0)
+        scatter(u10)
+        w2 = quantise_w(0, 512, g)
+        u20 = gated(2, 0, multiply(2, 0, w2), "g")
+        g = group_w(4, 0, 512, 0)
+        scatter(u12)
+        u22 = gated(2, 2, multiply(2, 2, w2), "g")
+        scatter(u20)
+        w3 = quantise_w(0, 512, g)
+        u30 = gated(3, 0, multiply(3, 0, w3), "g")
+        u32 = gated(3, 2, multiply(3, 2, w3), "g")
+        scatter(u30[:1])
+        finish(nc.gpsimd, 0)
+        scatter(u30[1:])
+        finish(nc.gpsimd, 1)
+        scatter(u22[:1])
+        scatter(u32[:1])
+        finish(nc.gpsimd, 2)
+        scatter(u22[1:])
+        scatter(u32[1:])
+        finish(nc.vector, 3)

@@ -42,7 +42,7 @@ def tile_moe_res_lin_none_kernel(tc, xT, xr, w, gate, offs, out):
         g_codes = [keep.tile([P, S], U32, name=f"g_codes{c}", align_bytes=64) for c in range(PASSES)]
         g_scales = keep.tile([P, S], U8, name="g_scales", align_bytes=64)
         window = [keep.tile([P, T], F32, name=f"window{t}") for t in range(NT)]
-        gates = [keep.tile([P, NT, C], F32, name=f"gates{e}") for e in range(E)]
+        gates = {}
         res = {}
 
         nc.gpsimd.memset(x_scales[:], 0)
@@ -57,18 +57,19 @@ def tile_moe_res_lin_none_kernel(tc, xT, xr, w, gate, offs, out):
             )
             return raw
 
-        def load_w(e, lo, hi):
-            raws = []
-            for c in range(PASSES):
-                raw = stage.tile([P, PACK, hi - lo], F32, name="raw")
-                nc.sync.dma_start(
-                    raw[:], w[e, c * KP : (c + 1) * KP, lo:hi].rearrange("(p j) n -> p j n", j=PACK)
-                )
-                raws.append(raw)
-            return raws
+        def load_w(e, c, lo=0, hi=N):
+            raw = stage.tile([P, PACK, hi - lo], F32, name="raw")
+            nc.sync.dma_start(
+                raw[:], w[e, c * KP : (c + 1) * KP, lo:hi].rearrange("(p j) n -> p j n", j=PACK)
+            )
+            return raw
 
-        def load_gate(e):
-            nc.sync.dma_start(gates[e][:], gate[:, e * C : (e + 1) * C].rearrange("(t p) s -> p t s", p=P))
+        def load_gate(e, t0):
+            gates[e, t0] = keep.tile([P, 2, C], F32, name=f"gate{e}{t0}")
+            nc.sync.dma_start(
+                gates[e, t0][:],
+                gate[t0 * P : (t0 + 2) * P, e * C : (e + 1) * C].rearrange("(t p) s -> p t s", p=P),
+            )
 
         def load_res(t):
             res[t] = stage.tile([P, T], F32, name="raw")
@@ -123,7 +124,7 @@ def tile_moe_res_lin_none_kernel(tc, xT, xr, w, gate, offs, out):
 
         def gated(e, t0, acc, how):
             y = yp.tile([P, 2, C], F32, name="y")
-            g = gates[e][:, t0 : t0 + 2, :]
+            g = gates[e, t0][:]
             if how == "v":
                 nc.vector.tensor_tensor(y[:], acc[:], g, MULT)
             elif how == "d":
@@ -138,78 +139,85 @@ def tile_moe_res_lin_none_kernel(tc, xT, xr, w, gate, offs, out):
             for e, t, values, how in items:
                 spots = window[t][:].indirect(offsets[:, e * C // 16 : (e + 1) * C // 16])
                 if how == "d":
-                    nc.vector.tensor_tensor(spots, values, gates[e][:, t, :], MULT)
+                    nc.vector.tensor_tensor(spots, values, gates[e, t - t % 2][:, t % 2, :], MULT)
                 else:
                     nc.vector.tensor_copy(spots, values)
 
-        def finish(engine, t):
-            engine.tensor_tensor(res[t][:], window[t][:], res[t][:], ADD)
-            nc.sync.dma_start(out[t * P : (t + 1) * P, :], res[t][:])
+        def finish(t, cuts):
+            for a, b in zip(cuts[:-1], cuts[1:]):
+                nc.vector.tensor_tensor(res[t][:, a:b], window[t][:, a:b], res[t][:, a:b], ADD)
+                nc.sync.dma_start(out[t * P : (t + 1) * P, a:b], res[t][:, a:b])
 
         x_at = [(c, t) for c in range(PASSES) for t in range(T // XC)]
         x_raw = [load_x(c, t) for c, t in x_at]
-        w_raw = {}
-        w_raw[0] = load_w(0, 0, 256)
-        load_gate(0)
-        w_raw[1] = load_w(0, 256, 512)
-        w_raw[2] = load_w(1, 0, 512)
-        load_gate(1)
+        w0a_raw = [load_w(0, c, 0, 256) for c in range(PASSES)]
+        load_gate(0, 0)
+        w0b_raw = [load_w(0, c, 256, 512) for c in range(PASSES)]
+        w1_raw = [load_w(1, c) for c in range(PASSES)]
+        w2_raw = []
+        w3_raw = []
         before = None
         for i in range(len(x_at)):
-            grouped = interleave(x_raw[i], XC, [256, 128, 128, 128, 128, 192][i])
+            grouped = interleave(x_raw[i], XC, [256, 128, 128, 128, 128, 256][i])
             if before:
                 quantise_x(*before)
             before = (*x_at[i], grouped)
             if i == 3:
                 gather(g_codes[0], x_codes[0], 0, S)
-                w_raw[3] = load_w(2, 0, 512)
-                load_gate(2)
+                w2_raw.append(load_w(2, 0))
+                load_gate(0, 2)
+                w2_raw.append(load_w(2, 1))
+                load_gate(1, 0)
             if i == 5:
-                w_raw[4] = load_w(3, 0, 512)
-                load_gate(3)
+                w3_raw.append(load_w(3, 0))
+                load_gate(1, 2)
+                w3_raw.append(load_w(3, 1))
+                load_gate(2, 0)
         quantise_x(*before)
         gather(g_scales, x_scales, 0, C)
         gather(g_codes[1], x_codes[1], 0, C)
 
-        def group_w(k, lo, hi, v):
-            return [interleave(w_raw[k][c], hi - lo, v) for c in range(PASSES)]
+        def group_w(raw, width, v):
+            return [interleave(raw[c], width, v) for c in range(PASSES)]
 
-        g = group_w(0, 0, 256, 64)
+        g = group_w(w0a_raw, 256, 64)
         w0a = quantise_w(0, 256, g)
-        u00 = gated(0, 0, multiply(0, 0, w0a), "v")
-        g = group_w(1, 256, 512, 0)
-        for t in range(NT):
-            load_res(t)
+        u00 = gated(0, 0, multiply(0, 0, w0a), "d")
+        g = group_w(w0b_raw, 256, 0)
+        load_res(0)
+        load_res(1)
+        load_gate(2, 2)
+        load_gate(3, 0)
+        load_gate(3, 2)
+        load_res(2)
+        load_res(3)
         w0b = quantise_w(256, 512, g)
-        gather(g_scales, x_scales, C, 2 * C)
-        gather(g_codes[1], x_codes[1], C, 2 * C)
-        u02 = gated(0, 2, multiply(0, 2, w0b), "g")
+        for lo in ((C, 2 * C), (2 * C, 4 * C)):
+            gather(g_scales, x_scales, *lo)
+            gather(g_codes[1], x_codes[1], *lo)
         scatter(u00)
-        g = group_w(2, 0, 512, 0)
-        gather(g_scales, x_scales, 2 * C, 4 * C)
-        gather(g_codes[1], x_codes[1], 2 * C, 4 * C)
-        w1 = quantise_w(0, 512, g)
-        u10 = gated(1, 0, multiply(1, 0, w1), "g")
+        u02 = gated(0, 2, multiply(0, 2, w0b), "d")
+        g = group_w(w1_raw, N, 128)
+        w1 = quantise_w(0, N, g)
         scatter(u02)
-        u12 = gated(1, 2, multiply(1, 2, w1), "g")
-        g = group_w(3, 0, 512, 0)
+        u10 = gated(1, 0, multiply(1, 0, w1), "d")
+        g = group_w(w2_raw, N, 0)
         scatter(u10)
-        w2 = quantise_w(0, 512, g)
-        u20 = gated(2, 0, multiply(2, 0, w2), "g")
-        g = group_w(4, 0, 512, 0)
+        u12 = gated(1, 2, multiply(1, 2, w1), "d")
+        w2 = quantise_w(0, N, g)
         scatter(u12)
-        u22 = gated(2, 2, multiply(2, 2, w2), "g")
+        u20 = gated(2, 0, multiply(2, 0, w2), "d")
+        g = group_w(w3_raw, N, 0)
         scatter(u20)
-        w3 = quantise_w(0, 512, g)
-        u30 = gated(3, 0, multiply(3, 0, w3), "g")
-        u32 = gated(3, 2, multiply(3, 2, w3), "g")
-        scatter(u30[:1])
-        finish(nc.gpsimd, 0)
-        scatter(u30[1:])
-        finish(nc.gpsimd, 1)
-        scatter(u22[:1])
+        u22 = gated(2, 2, multiply(2, 2, w2), "d")
+        w3 = quantise_w(0, N, g)
+        scatter(u22)
+        u30 = gated(3, 0, multiply(3, 0, w3), "d")
+        u32 = gated(3, 2, multiply(3, 2, w3), "d")
+        scatter(u30)
+        finish(0, (0, T))
         scatter(u32[:1])
-        finish(nc.gpsimd, 2)
-        scatter(u22[1:])
+        finish(1, (0, T))
         scatter(u32[1:])
-        finish(nc.vector, 3)
+        finish(2, (0, T))
+        finish(3, (0, T // 2, T))

@@ -21,17 +21,28 @@ KP = P * PACK
 PASSES = K // KP
 XC = 512
 NT = N // P
+STAGE = 10
+XLOADS = [[0,0,512],[0,512,1536],[1,0,1024],[1,1024,1536]]
+XSMALL = 2
+FIN = ["gg","gg","gv","vv"]
+GB = 3
+VX = [320,256,256,128,320,192]
+VW = [0,0,0,64]
+HOW = ["d","d","d","d","g","g","g","g"]
+ORDER = [["x",0,0],["x",1,0],["x",2,0],["x",3,0],["w",0,0],["w",0,1],["w",1,0],["g",1,0],["g",0,2],["w",1,1],["w",2,0],["g",0,0],["w",2,1],["w",3,0],["gp",0,0],["w",3,1],["gp",1,0],["r",1,0],["g",1,2],["gp",2,0],["gp",3,0],["r",0,0],["r",2,0],["r",3,0]]
 
 
 def tile_moe_res_lin_none_kernel(tc, xT, xr, w, gate, offs, out):
     nc = tc.nc
     with ExitStack() as ctx:
         keep = ctx.enter_context(tc.tile_pool(name="keep", bufs=1))
-        stage = ctx.enter_context(tc.tile_pool(name="stage", bufs=12))
+        stage = ctx.enter_context(tc.tile_pool(name="stage", bufs=10))
+        wide = ctx.enter_context(tc.tile_pool(name="wide", bufs=2))
         groups = ctx.enter_context(tc.tile_pool(name="groups", bufs=5))
+        slots = ctx.enter_context(tc.tile_pool(name="slots", bufs=GB))
         wq = ctx.enter_context(tc.tile_pool(name="wq", bufs=4))
         yp = ctx.enter_context(tc.tile_pool(name="yp", bufs=5))
-        zp = ctx.enter_context(tc.tile_pool(name="zp", bufs=3))
+        zp = ctx.enter_context(tc.tile_pool(name="zp", bufs=4))
         psum = ctx.enter_context(tc.psum_pool(name="psum", bufs=8))
 
         offsets = keep.tile([P, S // 16], U16, name="offsets")
@@ -39,8 +50,7 @@ def tile_moe_res_lin_none_kernel(tc, xT, xr, w, gate, offs, out):
 
         x_codes = [keep.tile([P, T], U32, name=f"x_codes{c}", align_bytes=64) for c in range(PASSES)]
         x_scales = keep.tile([P, T], U8, name="x_scales", align_bytes=64)
-        g_codes = [keep.tile([P, S], U32, name=f"g_codes{c}", align_bytes=64) for c in range(PASSES)]
-        g_scales = keep.tile([P, S], U8, name="g_scales", align_bytes=64)
+        g_codes0 = keep.tile([P, S], U32, name="g_codes0", align_bytes=64)
         window = [keep.tile([P, T], F32, name=f"window{t}") for t in range(NT)]
         gates = {}
         res = {}
@@ -49,13 +59,12 @@ def tile_moe_res_lin_none_kernel(tc, xT, xr, w, gate, offs, out):
         for t in range(NT):
             nc.gpsimd.memset(window[t][:], 0.0)
 
-        def load_x(c, t):
-            raw = stage.tile([P, PACK, XC], F32, name="raw")
-            nc.sync.dma_start(
-                raw[:],
-                xT[c * KP : (c + 1) * KP, t * XC : (t + 1) * XC].rearrange("(p j) w -> p j w", j=PACK),
-            )
-            return raw
+        def load_x(c, lo, hi):
+            pool = wide if hi - lo > XC else stage
+            raw = pool.tile([P, PACK, hi - lo], F32, name="x_raw" if hi - lo > XC else "raw")
+            nc.sync.dma_start(raw[:], xT[c * KP : (c + 1) * KP, lo:hi].rearrange("(p j) w -> p j w", j=PACK))
+            for a in range(lo, hi, XC):
+                x_parts.append((c, a // XC, raw, a - lo))
 
         def load_w(e, c, lo=0, hi=N):
             raw = stage.tile([P, PACK, hi - lo], F32, name="raw")
@@ -75,13 +84,13 @@ def tile_moe_res_lin_none_kernel(tc, xT, xr, w, gate, offs, out):
             res[t] = stage.tile([P, T], F32, name="raw")
             nc.sync.dma_start(res[t][:], xr[t * P : (t + 1) * P, :])
 
-        def interleave(raw, width, v):
+        def interleave(raw, width, v, base=0):
             grouped = groups.tile([P, width, PACK], BF16, name="grouped", align_bytes=64)
             for copy, a, b in ((nc.vector.tensor_copy, 0, v), (nc.scalar.copy, v, width)):
                 if a < b:
                     copy(
                         out=grouped[:, a:b, :].rearrange("p (c i) j -> p c j i", i=4),
-                        in_=raw[:, :, a:b].rearrange("p j (c i) -> p c j i", i=4),
+                        in_=raw[:, :, base + a : base + b].rearrange("p j (c i) -> p c j i", i=4),
                     )
             return grouped
 
@@ -95,7 +104,14 @@ def tile_moe_res_lin_none_kernel(tc, xT, xr, w, gate, offs, out):
             quantise(x_codes[c][:, cols], x_scales[4 * c :, cols], grouped)
 
         def gather(dst, src, lo, hi):
-            nc.vector.tensor_copy(dst[:, lo:hi], src[:].indirect(offsets[:, lo // 16 : hi // 16]))
+            nc.vector.tensor_copy(dst, src[:].indirect(offsets[:, lo // 16 : hi // 16]))
+
+        def gather_expert(e):
+            codes = slots.tile([P, C], U32, name="slot_codes", align_bytes=64)
+            scales = slots.tile([P, C], U8, name="slot_scales", align_bytes=64)
+            gather(scales[:], x_scales, e * C, (e + 1) * C)
+            gather(codes[:], x_codes[1], e * C, (e + 1) * C)
+            return (g_codes0[:, e * C : (e + 1) * C], codes[:]), scales
 
         def quantise_w(lo, hi, grouped):
             codes = wq.tile([P, PASSES, hi - lo], U32, name="w_codes", align_bytes=64)
@@ -104,22 +120,25 @@ def tile_moe_res_lin_none_kernel(tc, xT, xr, w, gate, offs, out):
                 quantise(codes[:, c, :], scales[:, c, :], grouped[c])
             return codes, scales, lo
 
-        def multiply(e, t0, tiles):
+        def multiply(acc, t, x_tiles, w_tiles):
+            x_words, x_bytes = x_tiles
+            codes, scales, lo = w_tiles
+            n_cols = slice(t * P, (t + 1) * P)
+            for c in range(PASSES):
+                nc.tensor.matmul_mx(
+                    out=acc,
+                    lhsT=codes[:, c, n_cols].bitcast(FP8X4),
+                    lhsT_scale=scales[:, c, n_cols],
+                    rhs=x_words[c].bitcast(FP8X4),
+                    rhs_scale=x_bytes[4 * c :, :],
+                    start=(c == 0),
+                    stop=(c == PASSES - 1),
+                )
+
+        def multiply_two(t0, x_tiles, w_tiles):
             acc = psum.tile([P, 2, C], F32, name="acc")
-            codes, scales, lo = tiles
-            slots = slice(e * C, (e + 1) * C)
             for i in range(2):
-                n_cols = slice((t0 + i) * P - lo, (t0 + i + 1) * P - lo)
-                for c in range(PASSES):
-                    nc.tensor.matmul_mx(
-                        out=acc[:, i, :],
-                        lhsT=codes[:, c, n_cols].bitcast(FP8X4),
-                        lhsT_scale=scales[:, c, n_cols],
-                        rhs=g_codes[c][:, slots].bitcast(FP8X4),
-                        rhs_scale=g_scales[4 * c :, slots],
-                        start=(c == 0),
-                        stop=(c == PASSES - 1),
-                    )
+                multiply(acc[:, i, :], t0 + i, x_tiles, w_tiles)
             return acc
 
         def gated(e, t0, acc, how):
@@ -135,6 +154,27 @@ def tile_moe_res_lin_none_kernel(tc, xT, xr, w, gate, offs, out):
                 nc.gpsimd.tensor_tensor(y[:], z[:], g, MULT)
             return [(e, t0 + i, y[:, i, :], how) for i in range(2)]
 
+        def load_gate_pair(t):
+            gates[t] = keep.tile([P, 2, C], F32, name=f"gate_pair{t}")
+            nc.sync.dma_start(
+                gates[t][:].rearrange("p e s -> p (e s)"), gate[t * P : (t + 1) * P, 2 * C :]
+            )
+
+        def gated_pair(t, acc, how):
+            y = yp.tile([P, 2, C], F32, name="y")
+            if how == "v":
+                nc.vector.tensor_tensor(y[:], acc[:], gates[t][:], MULT)
+            else:
+                z = zp.tile([P, 2, C], F32, name="z")
+                nc.scalar.copy(z[:], acc[:])
+                nc.gpsimd.tensor_tensor(y[:], z[:], gates[t][:], MULT)
+            return y
+
+        def scatter_pair(t, y):
+            nc.vector.tensor_copy(
+                window[t][:].indirect(offsets[:, 2 * C // 16 :]), y[:].rearrange("p e s -> p (e s)")
+            )
+
         def scatter(items):
             for e, t, values, how in items:
                 spots = window[t][:].indirect(offsets[:, e * C // 16 : (e + 1) * C // 16])
@@ -143,81 +183,75 @@ def tile_moe_res_lin_none_kernel(tc, xT, xr, w, gate, offs, out):
                 else:
                     nc.vector.tensor_copy(spots, values)
 
-        def finish(t, cuts):
+        def finish(t, cuts, engine=nc.vector):
             for a, b in zip(cuts[:-1], cuts[1:]):
-                nc.vector.tensor_tensor(res[t][:, a:b], window[t][:, a:b], res[t][:, a:b], ADD)
+                engine.tensor_tensor(res[t][:, a:b], window[t][:, a:b], res[t][:, a:b], ADD)
                 nc.sync.dma_start(out[t * P : (t + 1) * P, a:b], res[t][:, a:b])
 
-        x_at = [(c, t) for c in range(PASSES) for t in range(T // XC)]
-        x_raw = [load_x(c, t) for c, t in x_at]
-        w0a_raw = [load_w(0, c, 0, 256) for c in range(PASSES)]
-        load_gate(0, 0)
-        w0b_raw = [load_w(0, c, 256, 512) for c in range(PASSES)]
-        w1_raw = [load_w(1, c) for c in range(PASSES)]
-        w2_raw = []
-        w3_raw = []
+        x_parts = []
+        w_raw = {e: [] for e in range(E)}
+        queue = list(ORDER)
+        staged = [0]
+
+        def issue(used):
+            while queue:
+                kind, a, b = queue[0]
+                if kind != "g" and kind != "gp" and not (kind == "x" and XLOADS[a][2] - XLOADS[a][1] > XC):
+                    if staged[0] >= used + STAGE:
+                        return
+                    staged[0] += 1
+                queue.pop(0)
+                if kind == "x":
+                    load_x(*XLOADS[a])
+                elif kind == "w":
+                    w_raw[a].append(load_w(a, b))
+                elif kind == "g":
+                    load_gate(a, b)
+                elif kind == "gp":
+                    load_gate_pair(a)
+                else:
+                    load_res(a)
+
+        issue(0)
         before = None
-        for i in range(len(x_at)):
-            grouped = interleave(x_raw[i], XC, [256, 128, 128, 128, 128, 256][i])
+        for i, (c, t, raw, base) in enumerate(x_parts):
+            grouped = interleave(raw, XC, VX[i], base)
             if before:
                 quantise_x(*before)
-            before = (*x_at[i], grouped)
+            before = (c, t, grouped)
             if i == 3:
-                gather(g_codes[0], x_codes[0], 0, S)
-                w2_raw.append(load_w(2, 0))
-                load_gate(0, 2)
-                w2_raw.append(load_w(2, 1))
-                load_gate(1, 0)
-            if i == 5:
-                w3_raw.append(load_w(3, 0))
-                load_gate(1, 2)
-                w3_raw.append(load_w(3, 1))
-                load_gate(2, 0)
+                gather(g_codes0[:], x_codes[0], 0, S)
         quantise_x(*before)
-        gather(g_scales, x_scales, 0, C)
-        gather(g_codes[1], x_codes[1], 0, C)
+        issue(XSMALL)
 
-        def group_w(raw, width, v):
-            return [interleave(raw[c], width, v) for c in range(PASSES)]
+        def quantised_w(e):
+            tiles = quantise_w(0, N, [interleave(w_raw[e][c], N, VW[e]) for c in range(PASSES)])
+            issue(XSMALL + 2 * e + 2)
+            return tiles
 
-        g = group_w(w0a_raw, 256, 64)
-        w0a = quantise_w(0, 256, g)
-        u00 = gated(0, 0, multiply(0, 0, w0a), "d")
-        g = group_w(w0b_raw, 256, 0)
-        load_res(0)
-        load_res(1)
-        load_gate(2, 2)
-        load_gate(3, 0)
-        load_gate(3, 2)
-        load_res(2)
-        load_res(3)
-        w0b = quantise_w(256, 512, g)
-        for lo in ((C, 2 * C), (2 * C, 4 * C)):
-            gather(g_scales, x_scales, *lo)
-            gather(g_codes[1], x_codes[1], *lo)
+        x0 = gather_expert(0)
+        w0 = quantised_w(0)
+        u00 = gated(0, 0, multiply_two(0, x0, w0), HOW[0])
+        u02 = gated(0, 2, multiply_two(2, x0, w0), HOW[1])
+        x1 = gather_expert(1)
+        w1 = quantised_w(1)
+        u10 = gated(1, 0, multiply_two(0, x1, w1), HOW[2])
+        u12 = gated(1, 2, multiply_two(2, x1, w1), HOW[3])
+        x2 = gather_expert(2)
         scatter(u00)
-        u02 = gated(0, 2, multiply(0, 2, w0b), "d")
-        g = group_w(w1_raw, N, 128)
-        w1 = quantise_w(0, N, g)
         scatter(u02)
-        u10 = gated(1, 0, multiply(1, 0, w1), "d")
-        g = group_w(w2_raw, N, 0)
+        w2 = quantised_w(2)
+        accs = [psum.tile([P, 2, C], F32, name="acc") for t in range(NT)]
+        for t in range(NT):
+            multiply(accs[t][:, 0, :], t, x2, w2)
+        x3 = gather_expert(3)
         scatter(u10)
-        u12 = gated(1, 2, multiply(1, 2, w1), "d")
-        w2 = quantise_w(0, N, g)
         scatter(u12)
-        u20 = gated(2, 0, multiply(2, 0, w2), "d")
-        g = group_w(w3_raw, N, 0)
-        scatter(u20)
-        u22 = gated(2, 2, multiply(2, 2, w2), "d")
-        w3 = quantise_w(0, N, g)
-        scatter(u22)
-        u30 = gated(3, 0, multiply(3, 0, w3), "d")
-        u32 = gated(3, 2, multiply(3, 2, w3), "d")
-        scatter(u30)
-        finish(0, (0, T))
-        scatter(u32[:1])
-        finish(1, (0, T))
-        scatter(u32[1:])
-        finish(2, (0, T))
-        finish(3, (0, T // 2, T))
+        w3 = quantised_w(3)
+        for t in range(NT):
+            multiply(accs[t][:, 1, :], t, x3, w3)
+        ys = [gated_pair(t, accs[t], HOW[4 + t]) for t in range(NT)]
+        for t in range(NT):
+            scatter_pair(t, ys[t])
+            for h in range(2):
+                finish(t, (h * T // 2, (h + 1) * T // 2), nc.gpsimd if FIN[t][h] == "g" else nc.vector)

@@ -24,12 +24,12 @@ NT = N // P
 STAGE = 10
 XLOADS = [[0,0,512],[0,512,1536],[1,0,1024],[1,1024,1536]]
 XSMALL = 2
-FIN = ["gg","gg","gv","vv"]
+FIN = ["gg","gv","gg","vv"]
 GB = 3
-VX = [320,256,256,128,320,192]
-VW = [0,0,0,64]
-HOW = ["d","d","d","d","g","g","g","g"]
-ORDER = [["x",0,0],["x",1,0],["x",2,0],["x",3,0],["w",0,0],["w",0,1],["w",1,0],["g",1,0],["g",0,2],["w",1,1],["w",2,0],["g",0,0],["w",2,1],["w",3,0],["gp",0,0],["w",3,1],["gp",1,0],["r",1,0],["g",1,2],["gp",2,0],["gp",3,0],["r",0,0],["r",2,0],["r",3,0]]
+VX = [320,256,320,256,320,320]
+VW = [64,64,0,0]
+HOW = ["d","d","d","d","v","v","v","v"]
+ORDER = [["x",0,0],["x",1,0],["x",2,0],["x",3,0],["w",0,0],["w",0,1],["w",1,0],["g",0,0],["g",1,2],["w",1,1],["w",2,0],["g",0,2],["w",2,1],["w",3,0],["g",1,0],["w",3,1],["r",0,0],["gp",0,0],["gp",1,0],["gp",2,0],["r",3,0],["r",1,0],["r",2,0],["gp",3,0]]
 
 
 def tile_moe_res_lin_none_kernel(tc, xT, xr, w, gate, offs, out):
@@ -57,7 +57,7 @@ def tile_moe_res_lin_none_kernel(tc, xT, xr, w, gate, offs, out):
 
         nc.gpsimd.memset(x_scales[:], 0)
         for t in range(NT):
-            nc.gpsimd.memset(window[t][:], 0.0)
+            nc.vector.memset(window[t][:], 0.0)
 
         def load_x(c, lo, hi):
             pool = wide if hi - lo > XC else stage
@@ -164,16 +164,21 @@ def tile_moe_res_lin_none_kernel(tc, xT, xr, w, gate, offs, out):
             y = yp.tile([P, 2, C], F32, name="y")
             if how == "v":
                 nc.vector.tensor_tensor(y[:], acc[:], gates[t][:], MULT)
+            elif how == "d":
+                nc.scalar.copy(y[:], acc[:])
             else:
                 z = zp.tile([P, 2, C], F32, name="z")
                 nc.scalar.copy(z[:], acc[:])
                 nc.gpsimd.tensor_tensor(y[:], z[:], gates[t][:], MULT)
             return y
 
-        def scatter_pair(t, y):
-            nc.vector.tensor_copy(
-                window[t][:].indirect(offsets[:, 2 * C // 16 :]), y[:].rearrange("p e s -> p (e s)")
-            )
+        def scatter_pair(t, y, how):
+            spots = window[t][:].indirect(offsets[:, 2 * C // 16 :])
+            values = y[:].rearrange("p e s -> p (e s)")
+            if how == "d":
+                nc.vector.tensor_tensor(spots, values, gates[t][:].rearrange("p e s -> p (e s)"), MULT)
+            else:
+                nc.vector.tensor_copy(spots, values)
 
         def scatter(items):
             for e, t, values, how in items:
@@ -252,6 +257,6 @@ def tile_moe_res_lin_none_kernel(tc, xT, xr, w, gate, offs, out):
             multiply(accs[t][:, 1, :], t, x3, w3)
         ys = [gated_pair(t, accs[t], HOW[4 + t]) for t in range(NT)]
         for t in range(NT):
-            scatter_pair(t, ys[t])
+            scatter_pair(t, ys[t], HOW[4 + t])
             for h in range(2):
                 finish(t, (h * T // 2, (h + 1) * T // 2), nc.gpsimd if FIN[t][h] == "g" else nc.vector)

from contextlib import ExitStack

import concourse.mybir as mybir

K, T, E, C, N = 1024, 1536, 4, 256, 512
S = E * C
FLOPS = 2 * K * S * N

F32 = mybir.dt.float32
BF16 = mybir.dt.bfloat16
U32 = mybir.dt.uint32
U16 = mybir.dt.uint16
U8 = mybir.dt.uint8
FP8X4 = mybir.dt.float8_e4m3fn_x4
MULT = mybir.AluOpType.mult
ADD = mybir.AluOpType.add

P = 128
PACK = 4
KP = P * PACK
PASSES = K // KP
XC = 512
NT = N // P
STAGE = 10
XLOADS = [[0,0,512],[0,512,1536],[1,0,1024],[1,1024,1536]]
XSMALL = 2
FIN = ["gg","gv","gg","vv"]
GB = 3
VX = [320,256,320,256,320,320]
VW = [64,64,0,0]
HOW = ["d","d","d","d","v","v","v","v"]
ORDER = [["x",0,0],["x",1,0],["x",2,0],["x",3,0],["w",0,0],["w",0,1],["w",1,0],["g",0,0],["g",1,2],["w",1,1],["w",2,0],["g",0,2],["w",2,1],["w",3,0],["g",1,0],["w",3,1],["r",0,0],["gp",0,0],["gp",1,0],["gp",2,0],["r",3,0],["r",1,0],["r",2,0],["gp",3,0]]


def tile_moe_res_lin_none_kernel(tc, xT, xr, w, gate, offs, out):
    nc = tc.nc
    with ExitStack() as ctx:
        keep = ctx.enter_context(tc.tile_pool(name="keep", bufs=1))
        stage = ctx.enter_context(tc.tile_pool(name="stage", bufs=10))
        wide = ctx.enter_context(tc.tile_pool(name="wide", bufs=2))
        groups = ctx.enter_context(tc.tile_pool(name="groups", bufs=5))
        slots = ctx.enter_context(tc.tile_pool(name="slots", bufs=GB))
        wq = ctx.enter_context(tc.tile_pool(name="wq", bufs=4))
        yp = ctx.enter_context(tc.tile_pool(name="yp", bufs=5))
        zp = ctx.enter_context(tc.tile_pool(name="zp", bufs=4))
        psum = ctx.enter_context(tc.psum_pool(name="psum", bufs=8))

        offsets = keep.tile([P, S // 16], U16, name="offsets")
        nc.sync.dma_start(offsets[:], offs)

        x_codes = [keep.tile([P, T], U32, name=f"x_codes{c}", align_bytes=64) for c in range(PASSES)]
        x_scales = keep.tile([P, T], U8, name="x_scales", align_bytes=64)
        g_codes0 = keep.tile([P, S], U32, name="g_codes0", align_bytes=64)
        window = [keep.tile([P, T], F32, name=f"window{t}") for t in range(NT)]
        gates = {}
        res = {}

        nc.gpsimd.memset(x_scales[:], 0)
        for t in range(NT):
            nc.vector.memset(window[t][:], 0.0)

        def load_x(c, lo, hi):
            pool = wide if hi - lo > XC else stage
            raw = pool.tile([P, PACK, hi - lo], F32, name="x_raw" if hi - lo > XC else "raw")
            nc.sync.dma_start(raw[:], xT[c * KP : (c + 1) * KP, lo:hi].rearrange("(p j) w -> p j w", j=PACK))
            for a in range(lo, hi, XC):
                x_parts.append((c, a // XC, raw, a - lo))

        def load_w(e, c, lo=0, hi=N):
            raw = stage.tile([P, PACK, hi - lo], F32, name="raw")
            nc.sync.dma_start(
                raw[:], w[e, c * KP : (c + 1) * KP, lo:hi].rearrange("(p j) n -> p j n", j=PACK)
            )
            return raw

        def load_gate(e, t0):
            gates[e, t0] = keep.tile([P, 2, C], F32, name=f"gate{e}{t0}")
            nc.sync.dma_start(
                gates[e, t0][:],
                gate[t0 * P : (t0 + 2) * P, e * C : (e + 1) * C].rearrange("(t p) s -> p t s", p=P),
            )

        def load_res(t):
            res[t] = stage.tile([P, T], F32, name="raw")
            nc.sync.dma_start(res[t][:], xr[t * P : (t + 1) * P, :])

        def interleave(raw, width, v, base=0):
            grouped = groups.tile([P, width, PACK], BF16, name="grouped", align_bytes=64)
            for copy, a, b in ((nc.vector.tensor_copy, 0, v), (nc.scalar.copy, v, width)):
                if a < b:
                    copy(
                        out=grouped[:, a:b, :].rearrange("p (c i) j -> p c j i", i=4),
                        in_=raw[:, :, base + a : base + b].rearrange("p j (c i) -> p c j i", i=4),
                    )
            return grouped

        def quantise(codes, scales, grouped):
            nc.vector.quantize_mx(
                out=codes.bitcast(FP8X4), scales=scales, in_=grouped[:].rearrange("p w j -> p (w j)")
            )

        def quantise_x(c, t, grouped):
            cols = slice(t * XC, (t + 1) * XC)
            quantise(x_codes[c][:, cols], x_scales[4 * c :, cols], grouped)

        def gather(dst, src, lo, hi):
            nc.vector.tensor_copy(dst, src[:].indirect(offsets[:, lo // 16 : hi // 16]))

        def gather_expert(e):
            codes = slots.tile([P, C], U32, name="slot_codes", align_bytes=64)
            scales = slots.tile([P, C], U8, name="slot_scales", align_bytes=64)
            gather(scales[:], x_scales, e * C, (e + 1) * C)
            gather(codes[:], x_codes[1], e * C, (e + 1) * C)
            return (g_codes0[:, e * C : (e + 1) * C], codes[:]), scales

        def quantise_w(lo, hi, grouped):
            codes = wq.tile([P, PASSES, hi - lo], U32, name="w_codes", align_bytes=64)
            scales = wq.tile([P, PASSES, hi - lo], U8, name="w_scales", align_bytes=64)
            for c in range(PASSES):
                quantise(codes[:, c, :], scales[:, c, :], grouped[c])
            return codes, scales, lo

        def multiply(acc, t, x_tiles, w_tiles):
            x_words, x_bytes = x_tiles
            codes, scales, lo = w_tiles
            n_cols = slice(t * P, (t + 1) * P)
            for c in range(PASSES):
                nc.tensor.matmul_mx(
                    out=acc,
                    lhsT=codes[:, c, n_cols].bitcast(FP8X4),
                    lhsT_scale=scales[:, c, n_cols],
                    rhs=x_words[c].bitcast(FP8X4),
                    rhs_scale=x_bytes[4 * c :, :],
                    start=(c == 0),
                    stop=(c == PASSES - 1),
                )

        def multiply_two(t0, x_tiles, w_tiles):
            acc = psum.tile([P, 2, C], F32, name="acc")
            for i in range(2):
                multiply(acc[:, i, :], t0 + i, x_tiles, w_tiles)
            return acc

        def gated(e, t0, acc, how):
            y = yp.tile([P, 2, C], F32, name="y")
            g = gates[e, t0][:]
            if how == "v":
                nc.vector.tensor_tensor(y[:], acc[:], g, MULT)
            elif how == "d":
                nc.scalar.copy(y[:], acc[:])
            else:
                z = zp.tile([P, 2, C], F32, name="z")
                nc.scalar.copy(z[:], acc[:])
                nc.gpsimd.tensor_tensor(y[:], z[:], g, MULT)
            return [(e, t0 + i, y[:, i, :], how) for i in range(2)]

        def load_gate_pair(t):
            gates[t] = keep.tile([P, 2, C], F32, name=f"gate_pair{t}")
            nc.sync.dma_start(
                gates[t][:].rearrange("p e s -> p (e s)"), gate[t * P : (t + 1) * P, 2 * C :]
            )

        def gated_pair(t, acc, how):
            y = yp.tile([P, 2, C], F32, name="y")
            if how == "v":
                nc.vector.tensor_tensor(y[:], acc[:], gates[t][:], MULT)
            elif how == "d":
                nc.scalar.copy(y[:], acc[:])
            else:
                z = zp.tile([P, 2, C], F32, name="z")
                nc.scalar.copy(z[:], acc[:])
                nc.gpsimd.tensor_tensor(y[:], z[:], gates[t][:], MULT)
            return y

        def scatter_pair(t, y, how):
            spots = window[t][:].indirect(offsets[:, 2 * C // 16 :])
            values = y[:].rearrange("p e s -> p (e s)")
            if how == "d":
                nc.vector.tensor_tensor(spots, values, gates[t][:].rearrange("p e s -> p (e s)"), MULT)
            else:
                nc.vector.tensor_copy(spots, values)

        def scatter(items):
            for e, t, values, how in items:
                spots = window[t][:].indirect(offsets[:, e * C // 16 : (e + 1) * C // 16])
                if how == "d":
                    nc.vector.tensor_tensor(spots, values, gates[e, t - t % 2][:, t % 2, :], MULT)
                else:
                    nc.vector.tensor_copy(spots, values)

        def finish(t, cuts, engine=nc.vector):
            for a, b in zip(cuts[:-1], cuts[1:]):
                engine.tensor_tensor(res[t][:, a:b], window[t][:, a:b], res[t][:, a:b], ADD)
                nc.sync.dma_start(out[t * P : (t + 1) * P, a:b], res[t][:, a:b])

        x_parts = []
        w_raw = {e: [] for e in range(E)}
        queue = list(ORDER)
        staged = [0]

        def issue(used):
            while queue:
                kind, a, b = queue[0]
                if kind != "g" and kind != "gp" and not (kind == "x" and XLOADS[a][2] - XLOADS[a][1] > XC):
                    if staged[0] >= used + STAGE:
                        return
                    staged[0] += 1
                queue.pop(0)
                if kind == "x":
                    load_x(*XLOADS[a])
                elif kind == "w":
                    w_raw[a].append(load_w(a, b))
                elif kind == "g":
                    load_gate(a, b)
                elif kind == "gp":
                    load_gate_pair(a)
                else:
                    load_res(a)

        issue(0)
        before = None
        for i, (c, t, raw, base) in enumerate(x_parts):
            grouped = interleave(raw, XC, VX[i], base)
            if before:
                quantise_x(*before)
            before = (c, t, grouped)
            if i == 3:
                gather(g_codes0[:], x_codes[0], 0, S)
        quantise_x(*before)
        issue(XSMALL)

        def quantised_w(e):
            tiles = quantise_w(0, N, [interleave(w_raw[e][c], N, VW[e]) for c in range(PASSES)])
            issue(XSMALL + 2 * e + 2)
            return tiles

        x0 = gather_expert(0)
        w0 = quantised_w(0)
        u00 = gated(0, 0, multiply_two(0, x0, w0), HOW[0])
        u02 = gated(0, 2, multiply_two(2, x0, w0), HOW[1])
        x1 = gather_expert(1)
        w1 = quantised_w(1)
        u10 = gated(1, 0, multiply_two(0, x1, w1), HOW[2])
        u12 = gated(1, 2, multiply_two(2, x1, w1), HOW[3])
        x2 = gather_expert(2)
        scatter(u00)
        scatter(u02)
        w2 = quantised_w(2)
        accs = [psum.tile([P, 2, C], F32, name="acc") for t in range(NT)]
        for t in range(NT):
            multiply(accs[t][:, 0, :], t, x2, w2)
        x3 = gather_expert(3)
        scatter(u10)
        scatter(u12)
        w3 = quantised_w(3)
        for t in range(NT):
            multiply(accs[t][:, 1, :], t, x3, w3)
        ys = [gated_pair(t, accs[t], HOW[4 + t]) for t in range(NT)]
        for t in range(NT):
            scatter_pair(t, ys[t], HOW[4 + t])
            for h in range(2):
                finish(t, (h * T // 2, (h + 1) * T // 2), nc.gpsimd if FIN[t][h] == "g" else nc.vector)
